import numpy as np
import ml_dtypes


def mxq(x, axis, fmt="e4m3"):
    dtype, down = {"e4m3": (ml_dtypes.float8_e4m3fn, 7), "e5m2": (ml_dtypes.float8_e5m2, 14)}[fmt]
    v = np.moveaxis(np.asarray(x, np.float32).astype(ml_dtypes.bfloat16).astype(np.float64), axis, -1)
    blocks = v.reshape(v.shape[:-1] + (-1, 32))
    amax = np.abs(blocks).max(-1, keepdims=True)
    byte = np.maximum(np.where(amax > 0, np.frexp(amax)[1] - 1 + 127, 0) - down, 1)
    scale = np.exp2(byte - 127.0)
    codes = (blocks / scale).astype(np.float32).astype(dtype).astype(np.float64)
    return np.moveaxis((codes * scale).reshape(v.shape), -1, axis)


WIDE = False


def mx_kscale(k):
    if not WIDE:
        return np.ones(k)
    levels = np.array([10, -10, 5, -5, 0])
    if k % 512:
        return np.exp2(np.random.permutation(np.resize(levels, k // 32))).repeat(32)
    a = np.empty((k // 512, 16))
    for p in range(k // 512):
        a[p, :8] = np.random.permutation(np.resize(levels, 8))
        for g in range(8):
            far = levels[np.abs(levels - a[p, g]) >= 10]
            a[p, g + 8] = far[np.random.randint(len(far))]
    return np.exp2(a.ravel()).repeat(32)


def f64(x):
    return np.asarray(x).astype(np.float64)


def striped(idx):
    return np.tile(idx.reshape(-1, 16).T, (8, 1)).astype(np.uint16)


def unstriped(offs):
    return offs[:16].T.reshape(-1).astype(np.int64)


E2M1 = np.array([0.0, 0.5, 1.0, 1.5, 2.0, 3.0, 4.0, 6.0, -0.0, -0.5, -1.0, -1.5, -2.0, -3.0, -4.0, -6.0])


def pack_weight(w, fmt):
    k, n = w.shape
    w = f64(np.asarray(w, np.float32).astype(ml_dtypes.bfloat16)).reshape(k // 32, 32, n)
    amax = np.abs(w).max(1)
    if fmt == "e4m3":
        byte = np.frexp(amax)[1] - 1 + 127 - 7
    else:
        mant, ex = np.frexp(amax / 6.0)
        byte = np.where(mant > 0.5, ex, ex - 1) + 127
    byte = np.clip(np.where(amax > 0, byte, 1), 1, 254)
    scaled = (w * np.exp2(127.0 - byte)[:, None, :]).reshape(k, n).astype(np.float32)
    by_word = np.ascontiguousarray(scaled.reshape(k // 512, 128, 4, n).transpose(0, 1, 3, 2))
    if fmt == "e4m3":
        words = by_word.astype(ml_dtypes.float8_e4m3fn).view(np.uint8)
    else:
        c = by_word.astype(ml_dtypes.float4_e2m1fn).view(np.uint8) & 0xF
        words = (c[..., 0::2] | (c[..., 1::2] << 4)).reshape(k // 512, 128, 2 * n)
    return np.ascontiguousarray(words), np.ascontiguousarray(byte.astype(np.uint8).reshape(k // 512, 16, n))


def unpack_weight(words, scales, fmt):
    g, _, n = scales.shape
    words = np.ascontiguousarray(words).reshape(g, 128, n, -1)
    if fmt == "e4m3":
        vals = words.view(ml_dtypes.float8_e4m3fn).astype(np.float64)
    else:
        nib = np.empty((g, 128, n, 4), np.uint8)
        nib[..., 0::2] = words & 0xF
        nib[..., 1::2] = words >> 4
        vals = E2M1[nib]
    vals = vals * np.repeat(np.exp2(scales.astype(np.float64) - 127.0), 8, axis=1)[..., None]
    return vals.transpose(0, 1, 3, 2).reshape(g * 512, n)


def gelu(v):
    return 0.5 * v * (1.0 + np.tanh(np.sqrt(2.0 / np.pi) * (v + 0.044715 * v**3)))


K, K2, T, T3, S, P, H, N, R = 512, 1024, 4096, 2048, 1024, 512, 1024, 256, 128

def setup_inputs():
    n = np.random.standard_normal
    s = mx_kscale(K)[:, None]
    s2 = mx_kscale(K2)[:, None]
    u = mx_kscale(H)[:, None]
    d = {}
    d["tab_words"], d["tab_scales"] = pack_weight(n((K, T)) * s, "e4m3")
    d["tab2_words"], d["tab2_scales"] = pack_weight(n((K2, T3)) * s2, "e4m3")
    d["offs"] = striped(np.random.permutation(T)[:S])
    d["offs2"] = striped(np.random.permutation(T3)[:P])
    d["pos1"] = striped(np.random.permutation(S)[:P])
    d["w1"] = (n((K, H)) / K**0.5 / s).astype(np.float32)
    d["w2_words"], d["w2_scales"] = pack_weight(n((K, H)) / K**0.5 / s, "e2m1")
    d["w3_words"], d["w3_scales"] = pack_weight(2.0 * n((K2, H)) / K2**0.5 / s2, "e4m3")
    d["gain"] = (np.exp(0.3 * n(H)) * u[:, 0]).astype(np.float32)
    d["gb"] = (1.5 * np.exp(0.3 * n(H)) * u[:, 0]).astype(np.float32)
    d["wgs"] = np.exp(0.3 * n((R, P))).astype(np.float32)
    d["base"] = (n((H, S)) * u).astype(np.float32)
    d["w4"] = (0.42 * n((H, N)) / H**0.5 / u).astype(np.float32)
    return d

def reference(tab_words, tab_scales, tab2_words, tab2_scales, offs, offs2, pos1, w1, w2_words, w2_scales, w3_words, w3_scales, gain, gb, wgs, base, w4):
    v = unpack_weight(tab_words, tab_scales, "e4m3")[:, unstriped(offs)]
    v2 = unpack_weight(tab2_words, tab2_scales, "e4m3")[:, unstriped(offs2)]
    a1 = mxq(f64(w1), 0, "e4m3").T @ v
    a2 = unpack_weight(w2_words, w2_scales, "e2m1").T @ v
    a = np.minimum(a1, a2) * f64(gain)[:, None]
    f = unpack_weight(w3_words, w3_scales, "e4m3").T @ v2
    b = f / (1.0 + np.abs(f)) * f64(gb)[:, None]
    placed = np.zeros((H, S))
    placed[:, unstriped(pos1)] = np.tile(f64(wgs), (H // R, 1)) * b
    z = a + np.abs(placed - f64(base))
    y = mxq(f64(w4), 0, "e4m3").T @ mxq(z, 0, "e4m3")
    return np.sin(y)

@@ -1,0 +1,297 @@
+import math
+from contextlib import ExitStack
+
+import concourse.mybir as mybir
+from concourse.masks import make_identity
+
+FLOPS = 3758096384
+
+F32 = mybir.dt.float32
+BF16 = mybir.dt.bfloat16
+I32 = mybir.dt.int32
+U32 = mybir.dt.uint32
+U16 = mybir.dt.uint16
+U8 = mybir.dt.uint8
+FP8X4 = mybir.dt.float8_e4m3fn_x4
+FP4X4 = mybir.dt.float4_e2m1fn_x4
+ACT = mybir.ActivationFunctionType
+ALU = mybir.AluOpType
+
+P = 128
+T, T3, S, M, H, N = 4096, 2048, 1024, 512, 1024, 256
+QW = 256
+PAGES = 4
+W3_HEAD = 256
+
+
+def tile_list_chain_fault_scorer_kernel(
+    tc, tab_words, tab_scales, tab2_words, tab2_scales, offs, offs2, pos1,
+    w1, w2_words, w2_scales, w3_words, w3_scales, gain, gb, wgs, base, w4, out,
+):
+    nc = tc.nc
+    with ExitStack() as ctx:
+        keep = ctx.enter_context(tc.tile_pool(name="keep", bufs=1))
+        work = ctx.enter_context(tc.tile_pool(name="work", bufs=2))
+        psum = ctx.enter_context(tc.psum_pool(name="psum", bufs=1))
+
+        def words_of(packed):
+            return packed.rearrange("p c i -> p (c i)").bitcast(I32)
+
+        def load_plane(plane, scales, queue):
+            passes = scales.shape[0]
+            for quad in range(4):
+                rows = scales[:, 4 * quad : 4 * quad + 4, :].bitcast(I32)
+                if passes == 1:
+                    rows = rows[0]
+                queue.dma_start(out=plane[32 * quad : 32 * quad + 4 * passes, :].bitcast(I32), in_=rows)
+
+        offs_t = keep.tile([P, S // 16], U16, name="offs_t")
+        offs2_t = keep.tile([P, M // 16], U16, name="offs2_t")
+        pos1_t = keep.tile([P, M // 16], U16, name="pos1_t")
+        tab_w = keep.tile([P, T], I32, name="tab_w", align_bytes=64)
+        tab_s = keep.tile([P, T], U8, name="tab_s", align_bytes=64)
+        tab2_w = [keep.tile([P, T3], I32, name="tab2_w%d" % a, align_bytes=64) for a in range(2)]
+        tab2_s = keep.tile([P, T3], U8, name="tab2_s", align_bytes=64)
+        w3_head = keep.tile([P, 2, W3_HEAD], I32, name="w3_head", align_bytes=64)
+        w3_rest = keep.tile([P, 2, H - W3_HEAD], I32, name="w3_rest", align_bytes=64)
+        w3_s = keep.tile([P, H], U8, name="w3_s", align_bytes=64)
+        w2_raw = keep.tile([P, 2 * H], U8, name="w2_raw", align_bytes=64)
+        w2_sraw = keep.tile([P, H], U8, name="w2_sraw", align_bytes=64)
+        w2_w = keep.tile([P, 2 * H], U8, name="w2_w", align_bytes=64)
+        w2_s = keep.tile([P, H], U8, name="w2_s", align_bytes=64)
+        wgs_t = keep.tile([P, M], F32, name="wgs_t")
+        gain_t = keep.tile([P, 2, 4], F32, name="gain_t")
+        gb_rows = keep.tile([P, P], F32, name="gb_rows")
+        neg_gb = keep.tile([P, H // P], F32, name="neg_gb")
+        ident = keep.tile([P, P], F32, name="ident")
+        base_t = [keep.tile([P, S], F32, name="base%d" % i) for i in range(H // P)]
+        pages = [keep.tile([P, S], F32, name="page%d" % i) for i in range(PAGES)]
+        v_w = keep.tile([P, S], U32, name="v_w", align_bytes=64)
+        v_s = keep.tile([P, S], U8, name="v_s", align_bytes=64)
+        v2_w = [keep.tile([P, M], U32, name="v2_w%d" % a, align_bytes=64) for a in range(2)]
+        v2_s = keep.tile([P, M], U8, name="v2_s", align_bytes=64)
+        w1_w = [keep.tile([P, 512], U32, name="w1_w%d" % b, align_bytes=64) for b in range(2)]
+        w1_s = [keep.tile([P, 512], U8, name="w1_s%d" % b, align_bytes=64) for b in range(2)]
+        w4_w = keep.tile([P, 2, N], U32, name="w4_w", align_bytes=64)
+        w4_s = keep.tile([P, 2, N], U8, name="w4_s", align_bytes=64)
+
+        nc.vector.memset(tab2_s[:].bitcast(I32), 0)
+        nc.vector.memset(w3_s[:].bitcast(I32), 0)
+        nc.gpsimd.memset(gb_rows[:], 0.0)
+        nc.vector.memset(tab_s[:].bitcast(I32), 0)
+        nc.vector.memset(w2_sraw[:].bitcast(I32), 0)
+        make_identity(nc, ident[:])
+        for page in pages:
+            nc.vector.memset(page[:], 0.0)
+
+        nc.sync.dma_start(offs2_t[:], offs2)
+        nc.sync.dma_start(out=tab2_w[0][:], in_=words_of(tab2_words[0]))
+        load_plane(tab2_s, tab2_scales, nc.sync)
+        nc.sync.dma_start(out=tab2_w[1][:], in_=words_of(tab2_words[1]))
+        w3_all = w3_words.rearrange("a p c i -> p a (c i)").bitcast(I32)
+        nc.sync.dma_start(out=w3_head[:], in_=w3_all[:, :, :W3_HEAD])
+        nc.sync.dma_start(offs_t[:], offs)
+        load_plane(w3_s, w3_scales, nc.sync)
+        nc.gpsimd.dma_start(out=gb_rows[0 : H // P, :], in_=gb.rearrange("(i p) -> i p", p=P))
+        load_plane(tab_s, tab_scales, nc.gpsimd)
+        load_plane(w2_sraw, w2_scales, nc.gpsimd)
+        nc.gpsimd.dma_start(out=gain_t[:], in_=gain.rearrange("(b p t) -> p b t", p=P, t=4))
+        nc.sync.dma_start(pos1_t[:], pos1)
+        nc.sync.dma_start(out=wgs_t[:], in_=wgs)
+        nc.sync.dma_start(out=w3_rest[:], in_=w3_all[:, :, W3_HEAD:])
+        def load_base(i):
+            nc.sync.dma_start(out=base_t[i][:], in_=base[i * P : (i + 1) * P, :])
+
+        def load_w1(b):
+            raw = work.tile([P, 4, 512], F32, name="raw", tag="raw")
+            nc.sync.dma_start(out=raw[:], in_=w1[:, 512 * b : 512 * (b + 1)].rearrange("(p j) c -> p j c", j=4))
+            return raw
+
+        load_base(0)
+        load_base(1)
+        nc.sync.dma_start(out=tab_w[:], in_=words_of(tab_words[0]))
+        load_base(2)
+        load_base(3)
+        w1_raw = [load_w1(0)]
+        nc.sync.dma_start(out=w2_raw[:].bitcast(I32), in_=w2_words[0].bitcast(I32))
+        load_base(4)
+        load_base(5)
+        w1_raw.append(load_w1(1))
+        load_base(6)
+        load_base(7)
+
+        banks = [psum.tile([P, 512], F32, name="bank%d" % k) for k in range(8)]
+        turn = {"f": 0, "x": 0, "a2": 0, "d": 0}
+
+        def bank(role):
+            turn[role] = turn[role] + 1
+            return banks[2 * ("f", "x", "a2", "d").index(role) + turn[role] % 2]
+
+        gb_ps = bank("x")
+        nc.tensor.transpose(gb_ps[:, 0:P], gb_rows[:], ident[:])
+        nc.vector.tensor_scalar(neg_gb[:], gb_ps[:, 0 : H // P], -1.0, None, ALU.mult)
+
+        nc.vector.tensor_copy(v2_w[0][:], tab2_w[0][:].bitcast(U32).indirect(offs2_t[:]))
+        nc.vector.tensor_copy(v2_s[:], tab2_s[:].indirect(offs2_t[:]))
+        nc.vector.tensor_copy(v2_w[1][:], tab2_w[1][:].bitcast(U32).indirect(offs2_t[:]))
+        nc.vector.tensor_copy(v_s[:], tab_s[:].indirect(offs_t[:]))
+        nc.vector.tensor_copy(
+            out=w2_s[:].rearrange("p (b t m) -> p b t m", b=2, t=4),
+            in_=w2_sraw[:].rearrange("p (b m t) -> p b t m", b=2, t=4),
+        )
+
+        dist_t = {}
+
+        def place(i):
+            cols = slice(i * P, (i + 1) * P)
+            f_ps = bank("f")
+            for a in range(2):
+                if i * P < W3_HEAD:
+                    w3_w = w3_head[:, a, cols]
+                else:
+                    w3_w = w3_rest[:, a, i * P - W3_HEAD : (i + 1) * P - W3_HEAD]
+                nc.tensor.matmul_mx(
+                    out=f_ps[:], lhsT=w3_w.bitcast(FP8X4), lhsT_scale=w3_s[4 * a :, cols],
+                    rhs=v2_w[a][:].bitcast(FP8X4), rhs_scale=v2_s[4 * a :, :], start=(a == 0), stop=(a == 1),
+                )
+            size = work.tile([P, M], F32, name="size", tag="soft")
+            nc.scalar.activation(out=size[:], in_=f_ps[:], func=ACT.Abs)
+            root = work.tile([P, M], F32, name="root", tag="soft")
+            nc.scalar.activation(out=root[:], in_=size[:], func=ACT.Abs_reciprocal_sqrt, bias=1.0)
+            inv = work.tile([P, M], F32, name="inv")
+            nc.scalar.activation(out=inv[:], in_=root[:], func=ACT.Square)
+            neg_b = work.tile([P, M], F32, name="neg_b")
+            nc.vector.scalar_tensor_tensor(
+                out=neg_b[:], in0=f_ps[:], scalar=neg_gb[:, i : i + 1], in1=inv[:], op0=ALU.mult, op1=ALU.mult
+            )
+            page = pages[i % PAGES]
+            nc.vector.tensor_tensor(page[:].indirect(pos1_t[:]), neg_b[:], wgs_t[:], ALU.mult)
+            b, part = divmod(i, 4)
+            for half in range(2):
+                if part == 0:
+                    dist_t[b, half] = work.tile([P, 4, 4, P], F32, name="dist_t", tag="dist", bufs=4)
+                x_ps = bank("x")[:].rearrange("j (c r) -> j c r", c=4)
+                for c in range(4):
+                    jc = slice((4 * half + c) * P, (4 * half + c + 1) * P)
+                    nc.tensor.matmul(x_ps[:, c, :], base_t[i][:, jc], ident[:], start=True, stop=False, is_transpose=True)
+                    nc.tensor.matmul(x_ps[:, c, :], page[:, jc], ident[:], start=False, stop=True, is_transpose=True)
+                nc.scalar.activation(
+                    out=dist_t[b, half][:, :, :, 32 * part : 32 * (part + 1)],
+                    in_=x_ps.rearrange("j c (p t) -> j c t p", t=4), func=ACT.Abs,
+                )
+
+        def quantize_w1(b):
+            grouped = work.tile([P, 2048], BF16, name="grouped", tag="grouped", bufs=1, align_bytes=64)
+            nc.scalar.copy(
+                out=grouped[:].rearrange("p (t m j) -> p m t j", t=4, j=4),
+                in_=w1_raw[b][:].rearrange("p j (m t) -> p m t j", t=4),
+            )
+            nc.vector.quantize_mx(out=w1_w[b][:].bitcast(FP8X4), scales=w1_s[b][:], in_=grouped[:])
+
+        def quantize_w4():
+            raw = work.tile([P, 2, 4, N], F32, name="raw", tag="raw")
+            nc.sync.dma_start(
+                out=raw[:].rearrange("p b t n -> p b (t n)"), in_=w4.rearrange("(b p t) n -> p b (t n)", p=P, t=4)
+            )
+            grouped = work.tile([P, 2048], BF16, name="grouped", tag="grouped", bufs=1, align_bytes=64)
+            nc.scalar.copy(
+                out=grouped[:].rearrange("p (b n t) -> p b n t", b=2, t=4),
+                in_=raw[:].rearrange("p b t n -> p b n t"),
+            )
+            nc.vector.quantize_mx(
+                out=w4_w[:].rearrange("p b n -> p (b n)").bitcast(FP8X4),
+                scales=w4_s[:].rearrange("p b n -> p (b n)"), in_=grouped[:],
+            )
+
+        z_w, z_s = {}, {}
+
+        def make_z(b, q):
+            jc = slice(q * QW, (q + 1) * QW)
+            half, c0 = divmod(2 * q, 4)
+            planar = work.tile([P, 4, QW], BF16, name="planar", bufs=3)
+            for pair in range(2):
+                a1_ps, a2_ps, d_ps = (bank(role)[:].rearrange("p (u j) -> p u j", u=2) for role in ("f", "a2", "d"))
+                for u in range(2):
+                    t = 2 * pair + u
+                    nc.tensor.matmul_mx(
+                        out=a1_ps[:, u, :], lhsT=w1_w[b][:, t * P : (t + 1) * P].bitcast(FP8X4),
+                        lhsT_scale=w1_s[b][:, t * P : (t + 1) * P],
+                        rhs=v_w[:, jc].bitcast(FP8X4), rhs_scale=v_s[:, jc], start=True, stop=True,
+                    )
+                for u in range(2):
+                    c = 512 * b + (2 * pair + u) * P
+                    nc.tensor.matmul_mx(
+                        out=a2_ps[:, u, :], lhsT=w2_w[:, 2 * c : 2 * (c + P)].bitcast(FP4X4),
+                        lhsT_scale=w2_s[:, c : c + P],
+                        rhs=v_w[:, jc].bitcast(FP8X4), rhs_scale=v_s[:, jc], start=True, stop=True,
+                    )
+                for u in range(2):
+                    for c in range(2):
+                        nc.tensor.transpose(
+                            d_ps[:, u, c * P : (c + 1) * P], dist_t[b, half][:, c0 + c, 2 * pair + u, :], ident[:]
+                        )
+                a1 = work.tile([P, 2, QW], F32, name="a1", bufs=3)
+                nc.scalar.copy(out=a1[:], in_=a1_ps)
+                least = work.tile([P, 2, QW], F32, name="least", bufs=3)
+                nc.vector.tensor_tensor(least[:], a2_ps, a1[:], ALU.min)
+                for u in range(2):
+                    t = 2 * pair + u
+                    nc.vector.scalar_tensor_tensor(
+                        out=planar[:, t, :], in0=least[:, u, :], scalar=gain_t[:, b, t : t + 1], in1=d_ps[:, u, :],
+                        op0=ALU.mult, op1=ALU.add,
+                    )
+            woven = work.tile([P, QW, 4], BF16, name="woven", align_bytes=64)
+            weave = nc.vector.tensor_copy if (b, q) == (1, 3) else nc.scalar.copy
+            weave(out=woven[:], in_=planar[:].rearrange("p t j -> p j t"))
+            z_w[b, q] = work.tile([P, QW], U32, name="z_w", bufs=4, align_bytes=64)
+            z_s[b, q] = work.tile([P, QW], U8, name="z_s", bufs=4, align_bytes=64)
+            nc.vector.quantize_mx(
+                out=z_w[b, q][:].bitcast(FP8X4), scales=z_s[b, q][:], in_=woven[:].rearrange("p j t -> p (j t)")
+            )
+
+        out_v = out.rearrange("(a p) j -> p a j", p=P)
+
+        def score(q):
+            y_ps = bank("x")[:].rearrange("p (a j) -> p a j", a=2)
+            for a in range(2):
+                for b in range(2):
+                    nc.tensor.matmul_mx(
+                        out=y_ps[:, a, :], lhsT=w4_w[:, b, a * P : (a + 1) * P].bitcast(FP8X4),
+                        lhsT_scale=w4_s[:, b, a * P : (a + 1) * P],
+                        rhs=z_w[b, q][:].bitcast(FP8X4), rhs_scale=z_s[b, q][:], start=(b == 0), stop=(b == 1),
+                    )
+            parts = [slice(0, 1), slice(1, 2)] if q == 3 else [slice(0, 2)]
+            turns = work.tile([P, 2, QW], I32, name="turns")
+            angle = work.tile([P, 2, QW], F32, name="angle")
+            result = work.tile([P, 2, QW], F32, name="result")
+            for part in parts:
+                nc.vector.tensor_scalar(turns[:, part, :], y_ps[:, part, :], 1.0 / (2.0 * math.pi), None, ALU.mult)
+            for part in parts:
+                nc.vector.scalar_tensor_tensor(
+                    out=angle[:, part, :], in0=turns[:, part, :], scalar=-2.0 * math.pi, in1=y_ps[:, part, :],
+                    op0=ALU.mult, op1=ALU.add,
+                )
+                nc.scalar.activation(out=result[:, part, :], in_=angle[:, part, :], func=ACT.Sin)
+                nc.sync.dma_start(out=out_v[:, part, q * QW : (q + 1) * QW], in_=result[:, part, :])
+
+        for i in range(3):
+            place(i)
+        nc.vector.tensor_copy(v_w[:], tab_w[:].bitcast(U32).indirect(offs_t[:]))
+        place(3)
+        place(4)
+        quantize_w1(0)
+        nc.scalar.copy(
+            out=w2_w[:].bitcast(U16).rearrange("p (b t m) -> p b t m", b=2, t=4),
+            in_=w2_raw[:].bitcast(U16).rearrange("p (b m t) -> p b t m", b=2, t=4),
+        )
+        place(5)
+        quantize_w1(1)
+        place(6)
+        quantize_w4()
+        place(7)
+        make_z(0, 0)
+        for q in range(4):
+            if q < 3:
+                make_z(0, q + 1)
+            make_z(1, q)
+            score(q)

@@ -21,6 +21,7 @@ P = 128
 T, T3, S, M, H, N = 4096, 2048, 1024, 512, 1024, 256
 QW = 256
 PAGES = 4
+BASES = 7
 W3_HEAD = 256
 
 
@@ -37,20 +38,20 @@ def tile_list_chain_fault_scorer_kernel(
         def words_of(packed):
             return packed.rearrange("p c i -> p (c i)").bitcast(I32)
 
-        def load_plane(plane, scales, queue):
+        def load_plane(plane, scales, quads):
             passes = scales.shape[0]
-            for quad in range(4):
+            for quad in quads:
                 rows = scales[:, 4 * quad : 4 * quad + 4, :].bitcast(I32)
                 if passes == 1:
                     rows = rows[0]
-                queue.dma_start(out=plane[32 * quad : 32 * quad + 4 * passes, :].bitcast(I32), in_=rows)
+                nc.sync.dma_start(out=plane[32 * quad : 32 * quad + 4 * passes, :].bitcast(I32), in_=rows)
 
         offs_t = keep.tile([P, S // 16], U16, name="offs_t")
         offs2_t = keep.tile([P, M // 16], U16, name="offs2_t")
         pos1_t = keep.tile([P, M // 16], U16, name="pos1_t")
         tab_w = keep.tile([P, T], I32, name="tab_w", align_bytes=64)
         tab_s = keep.tile([P, T], U8, name="tab_s", align_bytes=64)
-        tab2_w = [keep.tile([P, T3], I32, name="tab2_w%d" % a, align_bytes=64) for a in range(2)]
+        tab2_w = [work.tile([P, T3], I32, name="tab2_w%d" % a, tag="early", align_bytes=64) for a in range(2)]
         tab2_s = keep.tile([P, T3], U8, name="tab2_s", align_bytes=64)
         w3_head = keep.tile([P, 2, W3_HEAD], I32, name="w3_head", align_bytes=64)
         w3_rest = keep.tile([P, 2, H - W3_HEAD], I32, name="w3_rest", align_bytes=64)
@@ -64,7 +65,7 @@ def tile_list_chain_fault_scorer_kernel(
         gb_rows = keep.tile([P, P], F32, name="gb_rows")
         neg_gb = keep.tile([P, H // P], F32, name="neg_gb")
         ident = keep.tile([P, P], F32, name="ident")
-        base_t = [keep.tile([P, S], F32, name="base%d" % i) for i in range(H // P)]
+        base_t = [keep.tile([P, S], F32, name="base%d" % i) for i in range(BASES)]
         pages = [keep.tile([P, S], F32, name="page%d" % i) for i in range(PAGES)]
         v_w = keep.tile([P, S], U32, name="v_w", align_bytes=64)
         v_s = keep.tile([P, S], U8, name="v_s", align_bytes=64)
@@ -79,28 +80,28 @@ def tile_list_chain_fault_scorer_kernel(
         nc.vector.memset(w3_s[:].bitcast(I32), 0)
         nc.gpsimd.memset(gb_rows[:], 0.0)
         nc.vector.memset(tab_s[:].bitcast(I32), 0)
-        nc.vector.memset(w2_sraw[:].bitcast(I32), 0)
         make_identity(nc, ident[:])
-        for page in pages:
-            nc.vector.memset(page[:], 0.0)
+        nc.gpsimd.memset(w2_sraw[:].bitcast(I32), 0)
+        for k, page in enumerate(pages):
+            (nc.vector if k < 2 else nc.gpsimd).memset(page[:].bitcast(I32), 0)
 
+        load_plane(tab2_s, tab2_scales, range(4))
         nc.sync.dma_start(offs2_t[:], offs2)
+        load_plane(w3_s, w3_scales, range(2))
         nc.sync.dma_start(out=tab2_w[0][:], in_=words_of(tab2_words[0]))
-        load_plane(tab2_s, tab2_scales, nc.sync)
+        load_plane(w3_s, w3_scales, range(2, 4))
+        nc.sync.dma_start(offs_t[:], offs)
         nc.sync.dma_start(out=tab2_w[1][:], in_=words_of(tab2_words[1]))
         w3_all = w3_words.rearrange("a p c i -> p a (c i)").bitcast(I32)
         nc.sync.dma_start(out=w3_head[:], in_=w3_all[:, :, :W3_HEAD])
-        nc.sync.dma_start(offs_t[:], offs)
-        load_plane(w3_s, w3_scales, nc.sync)
-        nc.gpsimd.dma_start(out=gb_rows[0 : H // P, :], in_=gb.rearrange("(i p) -> i p", p=P))
-        load_plane(tab_s, tab_scales, nc.gpsimd)
-        load_plane(w2_sraw, w2_scales, nc.gpsimd)
-        nc.gpsimd.dma_start(out=gain_t[:], in_=gain.rearrange("(b p t) -> p b t", p=P, t=4))
+        load_plane(tab_s, tab_scales, range(4))
+        nc.sync.dma_start(out=gb_rows[0 : H // P, :], in_=gb.rearrange("(i p) -> i p", p=P))
         nc.sync.dma_start(pos1_t[:], pos1)
         nc.sync.dma_start(out=wgs_t[:], in_=wgs)
         nc.sync.dma_start(out=w3_rest[:], in_=w3_all[:, :, W3_HEAD:])
+
         def load_base(i):
-            nc.sync.dma_start(out=base_t[i][:], in_=base[i * P : (i + 1) * P, :])
+            nc.sync.dma_start(out=base_t[i % BASES][:], in_=base[i * P : (i + 1) * P, :])
 
         def load_w1(b):
             raw = work.tile([P, 4, 512], F32, name="raw", tag="raw")
@@ -108,80 +109,83 @@ def tile_list_chain_fault_scorer_kernel(
             return raw
 
         load_base(0)
-        load_base(1)
         nc.sync.dma_start(out=tab_w[:], in_=words_of(tab_words[0]))
-        load_base(2)
-        load_base(3)
+        load_base(1)
+        load_plane(w2_sraw, w2_scales, range(4))
         w1_raw = [load_w1(0)]
         nc.sync.dma_start(out=w2_raw[:].bitcast(I32), in_=w2_words[0].bitcast(I32))
-        load_base(4)
-        load_base(5)
+        load_base(2)
+        nc.sync.dma_start(out=gain_t[:], in_=gain.rearrange("(b p t) -> p b t", p=P, t=4))
         w1_raw.append(load_w1(1))
-        load_base(6)
-        load_base(7)
+        load_base(3)
+        load_base(4)
+        w4_raw = keep.tile([P, 2, 4, N], F32, name="w4_raw")
+        nc.sync.dma_start(
+            out=w4_raw[:].rearrange("p b t n -> p b (t n)"), in_=w4.rearrange("(b p t) n -> p b (t n)", p=P, t=4)
+        )
+        for i in range(5, BASES):
+            load_base(i)
 
         banks = [psum.tile([P, 512], F32, name="bank%d" % k) for k in range(8)]
-        turn = {"f": 0, "x": 0, "a2": 0, "d": 0}
 
-        def bank(role):
-            turn[role] = turn[role] + 1
-            return banks[2 * ("f", "x", "a2", "d").index(role) + turn[role] % 2]
-
-        gb_ps = bank("x")
+        gb_ps = banks[7]
         nc.tensor.transpose(gb_ps[:, 0:P], gb_rows[:], ident[:])
         nc.vector.tensor_scalar(neg_gb[:], gb_ps[:, 0 : H // P], -1.0, None, ALU.mult)
 
-        nc.vector.tensor_copy(v2_w[0][:], tab2_w[0][:].bitcast(U32).indirect(offs2_t[:]))
         nc.vector.tensor_copy(v2_s[:], tab2_s[:].indirect(offs2_t[:]))
+        nc.vector.tensor_copy(v2_w[0][:], tab2_w[0][:].bitcast(U32).indirect(offs2_t[:]))
         nc.vector.tensor_copy(v2_w[1][:], tab2_w[1][:].bitcast(U32).indirect(offs2_t[:]))
         nc.vector.tensor_copy(v_s[:], tab_s[:].indirect(offs_t[:]))
-        nc.vector.tensor_copy(
-            out=w2_s[:].rearrange("p (b t m) -> p b t m", b=2, t=4),
-            in_=w2_sraw[:].rearrange("p (b m t) -> p b t m", b=2, t=4),
-        )
 
         dist_t = {}
 
-        def place(i):
+        f_ps, inv = {}, {}
+
+        def soften(i):
             cols = slice(i * P, (i + 1) * P)
-            f_ps = bank("f")
+            f_ps[i] = banks[i]
             for a in range(2):
                 if i * P < W3_HEAD:
                     w3_w = w3_head[:, a, cols]
                 else:
                     w3_w = w3_rest[:, a, i * P - W3_HEAD : (i + 1) * P - W3_HEAD]
                 nc.tensor.matmul_mx(
-                    out=f_ps[:], lhsT=w3_w.bitcast(FP8X4), lhsT_scale=w3_s[4 * a :, cols],
+                    out=f_ps[i][:], lhsT=w3_w.bitcast(FP8X4), lhsT_scale=w3_s[4 * a :, cols],
                     rhs=v2_w[a][:].bitcast(FP8X4), rhs_scale=v2_s[4 * a :, :], start=(a == 0), stop=(a == 1),
                 )
-            size = work.tile([P, M], F32, name="size", tag="soft")
-            nc.scalar.activation(out=size[:], in_=f_ps[:], func=ACT.Abs)
-            root = work.tile([P, M], F32, name="root", tag="soft")
-            nc.scalar.activation(out=root[:], in_=size[:], func=ACT.Abs_reciprocal_sqrt, bias=1.0)
-            inv = work.tile([P, M], F32, name="inv")
-            nc.scalar.activation(out=inv[:], in_=root[:], func=ACT.Square)
-            neg_b = work.tile([P, M], F32, name="neg_b")
+            inv[i] = keep.tile([P, M], F32, name="inv%d" % i)
+            nc.scalar.activation(out=inv[i][:], in_=f_ps[i][:], func=ACT.Abs)
+            nc.scalar.activation(out=inv[i][:], in_=inv[i][:], func=ACT.Abs_reciprocal_sqrt, bias=1.0)
+            nc.scalar.activation(out=inv[i][:], in_=inv[i][:], func=ACT.Square)
+
+        def place(i):
+            neg_b = inv[i]
             nc.vector.scalar_tensor_tensor(
-                out=neg_b[:], in0=f_ps[:], scalar=neg_gb[:, i : i + 1], in1=inv[:], op0=ALU.mult, op1=ALU.mult
+                out=neg_b[:], in0=f_ps[i][:], scalar=neg_gb[:, i : i + 1], in1=inv[i][:], op0=ALU.mult, op1=ALU.mult
             )
             page = pages[i % PAGES]
             nc.vector.tensor_tensor(page[:].indirect(pos1_t[:]), neg_b[:], wgs_t[:], ALU.mult)
+
+        def subtract(i):
+            page = pages[i % PAGES]
             b, part = divmod(i, 4)
             for half in range(2):
                 if part == 0:
                     dist_t[b, half] = work.tile([P, 4, 4, P], F32, name="dist_t", tag="dist", bufs=4)
-                x_ps = bank("x")[:].rearrange("j (c r) -> j c r", c=4)
+                x_ps = banks[(0, 2, 0, 2, 4, 0, 2, 4)[i] + half][:].rearrange("j (c r) -> j c r", c=4)
                 for c in range(4):
                     jc = slice((4 * half + c) * P, (4 * half + c + 1) * P)
-                    nc.tensor.matmul(x_ps[:, c, :], base_t[i][:, jc], ident[:], start=True, stop=False, is_transpose=True)
+                    nc.tensor.matmul(x_ps[:, c, :], base_t[i % BASES][:, jc], ident[:], start=True, stop=False, is_transpose=True)
                     nc.tensor.matmul(x_ps[:, c, :], page[:, jc], ident[:], start=False, stop=True, is_transpose=True)
                 nc.scalar.activation(
                     out=dist_t[b, half][:, :, :, 32 * part : 32 * (part + 1)],
                     in_=x_ps.rearrange("j c (p t) -> j c t p", t=4), func=ACT.Abs,
                 )
+            if i + BASES < H // P:
+                load_base(i + BASES)
 
         def quantize_w1(b):
-            grouped = work.tile([P, 2048], BF16, name="grouped", tag="grouped", bufs=1, align_bytes=64)
+            grouped = work.tile([P, 2048], BF16, name="w1_grouped", tag="early", align_bytes=64)
             nc.scalar.copy(
                 out=grouped[:].rearrange("p (t m j) -> p m t j", t=4, j=4),
                 in_=w1_raw[b][:].rearrange("p j (m t) -> p m t j", t=4),
@@ -189,109 +193,155 @@ def tile_list_chain_fault_scorer_kernel(
             nc.vector.quantize_mx(out=w1_w[b][:].bitcast(FP8X4), scales=w1_s[b][:], in_=grouped[:])
 
         def quantize_w4():
-            raw = work.tile([P, 2, 4, N], F32, name="raw", tag="raw")
-            nc.sync.dma_start(
-                out=raw[:].rearrange("p b t n -> p b (t n)"), in_=w4.rearrange("(b p t) n -> p b (t n)", p=P, t=4)
-            )
             grouped = work.tile([P, 2048], BF16, name="grouped", tag="grouped", bufs=1, align_bytes=64)
             nc.scalar.copy(
                 out=grouped[:].rearrange("p (b n t) -> p b n t", b=2, t=4),
-                in_=raw[:].rearrange("p b t n -> p b n t"),
+                in_=w4_raw[:].rearrange("p b t n -> p b n t"),
             )
             nc.vector.quantize_mx(
                 out=w4_w[:].rearrange("p b n -> p (b n)").bitcast(FP8X4),
                 scales=w4_s[:].rearrange("p b n -> p (b n)"), in_=grouped[:],
             )
 
-        z_w, z_s = {}, {}
+        blocks = [(0, 0, QW), (0, 256, QW), (0, 512, QW), (1, 0, QW), (0, 768, QW), (1, 256, QW), (1, 512, QW)]
+        blocks = blocks + [(1, 768, P), (1, 896, P)]
+        units = []
+        for k, (b, j0, width) in enumerate(blocks):
+            per = 512 // width
+            units.extend((k, range(t0, t0 + per)) for t0 in range(0, 4, per))
+        a1_ps, a2_ps, d_ps, a1, least, planar, woven, z_w, z_s = ({} for k in range(9))
 
-        def make_z(b, q):
-            jc = slice(q * QW, (q + 1) * QW)
-            half, c0 = divmod(2 * q, 4)
-            planar = work.tile([P, 4, QW], BF16, name="planar", bufs=3)
-            for pair in range(2):
-                a1_ps, a2_ps, d_ps = (bank(role)[:].rearrange("p (u j) -> p u j", u=2) for role in ("f", "a2", "d"))
-                for u in range(2):
-                    t = 2 * pair + u
-                    nc.tensor.matmul_mx(
-                        out=a1_ps[:, u, :], lhsT=w1_w[b][:, t * P : (t + 1) * P].bitcast(FP8X4),
-                        lhsT_scale=w1_s[b][:, t * P : (t + 1) * P],
-                        rhs=v_w[:, jc].bitcast(FP8X4), rhs_scale=v_s[:, jc], start=True, stop=True,
-                    )
-                for u in range(2):
-                    c = 512 * b + (2 * pair + u) * P
-                    nc.tensor.matmul_mx(
-                        out=a2_ps[:, u, :], lhsT=w2_w[:, 2 * c : 2 * (c + P)].bitcast(FP4X4),
-                        lhsT_scale=w2_s[:, c : c + P],
-                        rhs=v_w[:, jc].bitcast(FP8X4), rhs_scale=v_s[:, jc], start=True, stop=True,
-                    )
-                for u in range(2):
-                    for c in range(2):
-                        nc.tensor.transpose(
-                            d_ps[:, u, c * P : (c + 1) * P], dist_t[b, half][:, c0 + c, 2 * pair + u, :], ident[:]
-                        )
-                a1 = work.tile([P, 2, QW], F32, name="a1", bufs=3)
-                nc.scalar.copy(out=a1[:], in_=a1_ps)
-                least = work.tile([P, 2, QW], F32, name="least", bufs=3)
-                nc.vector.tensor_tensor(least[:], a2_ps, a1[:], ALU.min)
-                for u in range(2):
-                    t = 2 * pair + u
-                    nc.vector.scalar_tensor_tensor(
-                        out=planar[:, t, :], in0=least[:, u, :], scalar=gain_t[:, b, t : t + 1], in1=d_ps[:, u, :],
-                        op0=ALU.mult, op1=ALU.add,
-                    )
-            woven = work.tile([P, QW, 4], BF16, name="woven", align_bytes=64)
-            weave = nc.vector.tensor_copy if (b, q) == (1, 3) else nc.scalar.copy
-            weave(out=woven[:], in_=planar[:].rearrange("p t j -> p j t"))
-            z_w[b, q] = work.tile([P, QW], U32, name="z_w", bufs=4, align_bytes=64)
-            z_s[b, q] = work.tile([P, QW], U8, name="z_s", bufs=4, align_bytes=64)
+        def in_parts(tile, width):
+            return tile[:].rearrange("p (u j) -> p u j", j=width)
+
+        def multiply(n):
+            k, ts = units[n]
+            b, j0, width = blocks[k]
+            jc = slice(j0, j0 + width)
+            a1_ps[n] = in_parts(banks[n % 2], width)
+            a2_ps[n] = in_parts(banks[2 + n % 2], width)
+            for u, t in enumerate(ts):
+                nc.tensor.matmul_mx(
+                    out=a1_ps[n][:, u, :], lhsT=w1_w[b][:, t * P : (t + 1) * P].bitcast(FP8X4),
+                    lhsT_scale=w1_s[b][:, t * P : (t + 1) * P],
+                    rhs=v_w[:, jc].bitcast(FP8X4), rhs_scale=v_s[:, jc], start=True, stop=True,
+                )
+            for u, t in enumerate(ts):
+                c = 512 * b + t * P
+                nc.tensor.matmul_mx(
+                    out=a2_ps[n][:, u, :], lhsT=w2_w[:, 2 * c : 2 * (c + P)].bitcast(FP4X4),
+                    lhsT_scale=w2_s[:, c : c + P],
+                    rhs=v_w[:, jc].bitcast(FP8X4), rhs_scale=v_s[:, jc], start=True, stop=True,
+                )
+
+        def turn_back(n):
+            k, ts = units[n]
+            b, j0, width = blocks[k]
+            d_ps[n] = in_parts(banks[6 + n % 2], width)
+            for u, t in enumerate(ts):
+                for c in range(width // P):
+                    half, chunk = divmod(j0 // P + c, 4)
+                    nc.tensor.transpose(d_ps[n][:, u, c * P : (c + 1) * P], dist_t[b, half][:, chunk, t, :], ident[:])
+
+        def take_least(n):
+            width = blocks[units[n][0]][2]
+            a1[n] = in_parts(work.tile([P, 512], F32, name="a1", bufs=3), width)
+            nc.scalar.copy(out=a1[n], in_=a1_ps[n])
+            least[n] = in_parts(work.tile([P, 512], F32, name="least", bufs=3), width)
+            nc.vector.tensor_tensor(least[n], a2_ps[n], a1[n], ALU.min)
+
+        def join(n):
+            k, ts = units[n]
+            b, j0, width = blocks[k]
+            if ts[0] == 0:
+                planar[k] = work.tile([P, 4, width], BF16, name="planar", bufs=3)
+            for u, t in enumerate(ts):
+                nc.vector.scalar_tensor_tensor(
+                    out=planar[k][:, t, :], in0=least[n][:, u, :], scalar=gain_t[:, b, t : t + 1],
+                    in1=d_ps[n][:, u, :], op0=ALU.mult, op1=ALU.add,
+                )
+
+        def weave(k):
+            width = blocks[k][2]
+            woven[k] = work.tile([P, width, 4], BF16, name="woven", align_bytes=64)
+            copy = nc.vector.tensor_copy if k == len(blocks) - 1 else nc.scalar.copy
+            copy(out=woven[k][:], in_=planar[k][:].rearrange("p t j -> p j t"))
+
+        def quantize_z(k):
+            b, j0, width = blocks[k]
+            codes = work.tile([P, width], U32, name="z_w", bufs=5, align_bytes=64)
+            plane = work.tile([P, width], U8, name="z_s", bufs=5, align_bytes=64)
             nc.vector.quantize_mx(
-                out=z_w[b, q][:].bitcast(FP8X4), scales=z_s[b, q][:], in_=woven[:].rearrange("p j t -> p (j t)")
+                out=codes[:].bitcast(FP8X4), scales=plane[:], in_=woven[k][:].rearrange("p j t -> p (j t)")
             )
+            for c in range(0, width, P):
+                z_w[b, j0 + c], z_s[b, j0 + c] = codes[:, c:], plane[:, c:]
 
         out_v = out.rearrange("(a p) j -> p a j", p=P)
 
-        def score(q):
-            y_ps = bank("x")[:].rearrange("p (a j) -> p a j", a=2)
+        def score(k):
+            b, j0, width = blocks[k]
+            y_ps = in_parts(banks[5 if width == QW else 2 * (len(blocks) - 1 - k)], width)[:, 0:2, :]
             for a in range(2):
                 for b in range(2):
                     nc.tensor.matmul_mx(
                         out=y_ps[:, a, :], lhsT=w4_w[:, b, a * P : (a + 1) * P].bitcast(FP8X4),
                         lhsT_scale=w4_s[:, b, a * P : (a + 1) * P],
-                        rhs=z_w[b, q][:].bitcast(FP8X4), rhs_scale=z_s[b, q][:], start=(b == 0), stop=(b == 1),
+                        rhs=z_w[b, j0][:, :width].bitcast(FP8X4), rhs_scale=z_s[b, j0][:, :width],
+                        start=(b == 0), stop=(b == 1),
                     )
-            parts = [slice(0, 1), slice(1, 2)] if q == 3 else [slice(0, 2)]
-            turns = work.tile([P, 2, QW], I32, name="turns")
-            angle = work.tile([P, 2, QW], F32, name="angle")
-            result = work.tile([P, 2, QW], F32, name="result")
-            for part in parts:
-                nc.vector.tensor_scalar(turns[:, part, :], y_ps[:, part, :], 1.0 / (2.0 * math.pi), None, ALU.mult)
-            for part in parts:
-                nc.vector.scalar_tensor_tensor(
-                    out=angle[:, part, :], in0=turns[:, part, :], scalar=-2.0 * math.pi, in1=y_ps[:, part, :],
-                    op0=ALU.mult, op1=ALU.add,
-                )
-                nc.scalar.activation(out=result[:, part, :], in_=angle[:, part, :], func=ACT.Sin)
-                nc.sync.dma_start(out=out_v[:, part, q * QW : (q + 1) * QW], in_=result[:, part, :])
+            turns = work.tile([P, 2, width], I32, name="turns")
+            nc.vector.tensor_scalar(turns[:], y_ps, 1.0 / (2.0 * math.pi), None, ALU.mult)
+            angle = work.tile([P, 2, width], F32, name="angle")
+            nc.vector.scalar_tensor_tensor(
+                out=angle[:], in0=turns[:], scalar=-2.0 * math.pi, in1=y_ps, op0=ALU.mult, op1=ALU.add
+            )
+            result = work.tile([P, 2, width], F32, name="result", bufs=3)
+            nc.scalar.activation(out=result[:], in_=angle[:], func=ACT.Sin)
+            nc.sync.dma_start(out=out_v[:, :, j0 : j0 + width], in_=result[:])
 
-        for i in range(3):
-            place(i)
+        for i in range(6):
+            soften(i)
         nc.vector.tensor_copy(v_w[:], tab_w[:].bitcast(U32).indirect(offs_t[:]))
-        place(3)
-        place(4)
+        nc.vector.tensor_copy(
+            out=w2_s[:].rearrange("p (b t m) -> p b t m", b=2, t=4),
+            in_=w2_sraw[:].rearrange("p (b m t) -> p b t m", b=2, t=4),
+        )
         quantize_w1(0)
         nc.scalar.copy(
             out=w2_w[:].bitcast(U16).rearrange("p (b t m) -> p b t m", b=2, t=4),
             in_=w2_raw[:].bitcast(U16).rearrange("p (b m t) -> p b t m", b=2, t=4),
         )
-        place(5)
+        soften(6)
+        soften(7)
+        for i in range(H // P):
+            if i >= PAGES:
+                subtract(i - PAGES)
+            place(i)
         quantize_w1(1)
-        place(6)
+        subtract(4)
         quantize_w4()
-        place(7)
-        make_z(0, 0)
-        for q in range(4):
-            if q < 3:
-                make_z(0, q + 1)
-            make_z(1, q)
-            score(q)
+        subtract(5)
+        subtract(6)
+        multiply(0)
+        turn_back(0)
+        multiply(1)
+        take_least(0)
+        count = len(units)
+        ends = {n: k for n, (k, ts) in enumerate(units) if ts[-1] == 3}
+        for n in range(count + 2):
+            if n + 2 < count:
+                multiply(n + 2)
+            if n + 1 < count:
+                turn_back(n + 1)
+                take_least(n + 1)
+            if n < count:
+                join(n)
+            if n == 1:
+                subtract(7)
+            if n - 1 in ends:
+                weave(ends[n - 1])
+            if n - 2 in ends:
+                quantize_z(ends[n - 2])
+                if blocks[ends[n - 2]][0] == 1:
+                    score(ends[n - 2])

@@ -128,6 +128,8 @@ def tile_list_chain_fault_scorer_kernel(
 
         banks = [psum.tile([P, 512], F32, name="bank%d" % k) for k in range(8)]
 
+        spare = keep.tile([P, 2], F32, name="spare")
+        nc.scalar.activation(out=spare[:, 0:1], in_=ident[:, 0:1], func=ACT.Abs_reciprocal_sqrt, bias=1.0)
         gb_ps = banks[7]
         nc.tensor.transpose(gb_ps[:, 0:P], gb_rows[:], ident[:])
         nc.vector.tensor_scalar(neg_gb[:], gb_ps[:, 0 : H // P], -1.0, None, ALU.mult)
@@ -314,6 +316,7 @@ def tile_list_chain_fault_scorer_kernel(
         )
         soften(6)
         soften(7)
+        nc.scalar.activation(out=spare[:, 1:2], in_=inv[7][:, 0:1], func=ACT.Sin)
         for i in range(H // P):
             if i >= PAGES:
                 subtract(i - PAGES)

@@ -95,6 +95,7 @@ def tile_list_chain_fault_scorer_kernel(
         w3_all = w3_words.rearrange("a p c i -> p a (c i)").bitcast(I32)
         nc.sync.dma_start(out=w3_head[:], in_=w3_all[:, :, :W3_HEAD])
         load_plane(tab_s, tab_scales, range(4))
+        load_plane(w2_sraw, w2_scales, range(4))
         nc.sync.dma_start(out=gb_rows[0 : H // P, :], in_=gb.rearrange("(i p) -> i p", p=P))
         nc.sync.dma_start(pos1_t[:], pos1)
         nc.sync.dma_start(out=wgs_t[:], in_=wgs)
@@ -111,7 +112,6 @@ def tile_list_chain_fault_scorer_kernel(
         load_base(0)
         nc.sync.dma_start(out=tab_w[:], in_=words_of(tab_words[0]))
         load_base(1)
-        load_plane(w2_sraw, w2_scales, range(4))
         w1_raw = [load_w1(0)]
         nc.sync.dma_start(out=w2_raw[:].bitcast(I32), in_=w2_words[0].bitcast(I32))
         load_base(2)
@@ -174,11 +174,14 @@ def tile_list_chain_fault_scorer_kernel(
             for half in range(2):
                 if part == 0:
                     dist_t[b, half] = work.tile([P, 4, 4, P], F32, name="dist_t", tag="dist", bufs=4)
-                x_ps = banks[(0, 2, 0, 2, 4, 0, 2, 4)[i] + half][:].rearrange("j (c r) -> j c r", c=4)
-                for c in range(4):
-                    jc = slice((4 * half + c) * P, (4 * half + c + 1) * P)
-                    nc.tensor.matmul(x_ps[:, c, :], base_t[i % BASES][:, jc], ident[:], start=True, stop=False, is_transpose=True)
-                    nc.tensor.matmul(x_ps[:, c, :], page[:, jc], ident[:], start=False, stop=True, is_transpose=True)
+                x_ps = banks[(0, 2, 0, 2, 4, 0, 4, 4)[i] + half][:].rearrange("j (c r) -> j c r", c=4)
+                for step, source in enumerate((base_t[i % BASES], page)):
+                    for c in range(4):
+                        jc = slice((4 * half + c) * P, (4 * half + c + 1) * P)
+                        nc.tensor.matmul(
+                            x_ps[:, c, :], source[:, jc], ident[:],
+                            start=(step, c) == (0, 0), stop=(step, c) == (1, 3), is_transpose=True,
+                        )
                 nc.scalar.activation(
                     out=dist_t[b, half][:, :, :, 32 * part : 32 * (part + 1)],
                     in_=x_ps.rearrange("j c (p t) -> j c t p", t=4), func=ACT.Abs,
@@ -266,8 +269,13 @@ def tile_list_chain_fault_scorer_kernel(
         def weave(k):
             width = blocks[k][2]
             woven[k] = work.tile([P, width, 4], BF16, name="woven", align_bytes=64)
-            copy = nc.vector.tensor_copy if k == len(blocks) - 1 else nc.scalar.copy
-            copy(out=woven[k][:], in_=planar[k][:].rearrange("p t j -> p j t"))
+            stepped = planar[k][:].rearrange("p t j -> p j t")
+            if k < len(blocks) - 2:
+                nc.gpsimd.tensor_scalar(woven[k][:], stepped, 1.0, 0.0, ALU.mult, ALU.add)
+            elif k == len(blocks) - 1:
+                nc.vector.tensor_copy(out=woven[k][:], in_=stepped)
+            else:
+                nc.scalar.copy(out=woven[k][:], in_=stepped)
 
         def quantize_z(k):
             b, j0, width = blocks[k]
@@ -283,7 +291,7 @@ def tile_list_chain_fault_scorer_kernel(
 
         def score(k):
             b, j0, width = blocks[k]
-            y_ps = in_parts(banks[5 if width == QW else 2 * (len(blocks) - 1 - k)], width)[:, 0:2, :]
+            y_ps = in_parts(banks[4 + k % 2 if width == QW else 2 * (len(blocks) - 1 - k)], width)[:, 0:2, :]
             for a in range(2):
                 for b in range(2):
                     nc.tensor.matmul_mx(
@@ -293,12 +301,17 @@ def tile_list_chain_fault_scorer_kernel(
                         start=(b == 0), stop=(b == 1),
                     )
             turns = work.tile([P, 2, width], I32, name="turns")
-            nc.vector.tensor_scalar(turns[:], y_ps, 1.0 / (2.0 * math.pi), None, ALU.mult)
+            if j0 < 512:
+                staged = work.tile([P, 2, width], F32, name="staged", tag="raw")
+                nc.scalar.copy(out=staged[:], in_=y_ps)
+                nc.gpsimd.tensor_scalar(turns[:], staged[:], 1.0 / (2.0 * math.pi), 0.0, ALU.mult, ALU.add)
+            else:
+                nc.vector.tensor_scalar(turns[:], y_ps, 1.0 / (2.0 * math.pi), None, ALU.mult)
             angle = work.tile([P, 2, width], F32, name="angle")
             nc.vector.scalar_tensor_tensor(
                 out=angle[:], in0=turns[:], scalar=-2.0 * math.pi, in1=y_ps, op0=ALU.mult, op1=ALU.add
             )
-            result = work.tile([P, 2, width], F32, name="result", bufs=3)
+            result = work.tile([P, 2, width], F32, name="result", bufs=4)
             nc.scalar.activation(out=result[:], in_=angle[:], func=ACT.Sin)
             nc.sync.dma_start(out=out_v[:, :, j0 : j0 + width], in_=result[:])
 

import math
from contextlib import ExitStack

import concourse.mybir as mybir
from concourse.masks import make_identity

FLOPS = 3758096384

F32 = mybir.dt.float32
BF16 = mybir.dt.bfloat16
I32 = mybir.dt.int32
U32 = mybir.dt.uint32
U16 = mybir.dt.uint16
U8 = mybir.dt.uint8
FP8X4 = mybir.dt.float8_e4m3fn_x4
FP4X4 = mybir.dt.float4_e2m1fn_x4
ACT = mybir.ActivationFunctionType
ALU = mybir.AluOpType

P = 128
T, T3, S, M, H, N = 4096, 2048, 1024, 512, 1024, 256
QW = 256
PAGES = 4
BASES = 7
W3_HEAD = 256


def tile_list_chain_fault_scorer_kernel(
    tc, tab_words, tab_scales, tab2_words, tab2_scales, offs, offs2, pos1,
    w1, w2_words, w2_scales, w3_words, w3_scales, gain, gb, wgs, base, w4, out,
):
    nc = tc.nc
    with ExitStack() as ctx:
        keep = ctx.enter_context(tc.tile_pool(name="keep", bufs=1))
        work = ctx.enter_context(tc.tile_pool(name="work", bufs=2))
        psum = ctx.enter_context(tc.psum_pool(name="psum", bufs=1))

        def words_of(packed):
            return packed.rearrange("p c i -> p (c i)").bitcast(I32)

        def load_plane(plane, scales, quads):
            passes = scales.shape[0]
            for quad in quads:
                rows = scales[:, 4 * quad : 4 * quad + 4, :].bitcast(I32)
                if passes == 1:
                    rows = rows[0]
                nc.sync.dma_start(out=plane[32 * quad : 32 * quad + 4 * passes, :].bitcast(I32), in_=rows)

        offs_t = keep.tile([P, S // 16], U16, name="offs_t")
        offs2_t = keep.tile([P, M // 16], U16, name="offs2_t")
        pos1_t = keep.tile([P, M // 16], U16, name="pos1_t")
        tab_w = keep.tile([P, T], I32, name="tab_w", align_bytes=64)
        tab_s = keep.tile([P, T], U8, name="tab_s", align_bytes=64)
        tab2_w = [work.tile([P, T3], I32, name="tab2_w%d" % a, tag="early", align_bytes=64) for a in range(2)]
        tab2_s = keep.tile([P, T3], U8, name="tab2_s", align_bytes=64)
        w3_head = keep.tile([P, 2, W3_HEAD], I32, name="w3_head", align_bytes=64)
        w3_rest = keep.tile([P, 2, H - W3_HEAD], I32, name="w3_rest", align_bytes=64)
        w3_s = keep.tile([P, H], U8, name="w3_s", align_bytes=64)
        w2_raw = keep.tile([P, 2 * H], U8, name="w2_raw", align_bytes=64)
        w2_sraw = keep.tile([P, H], U8, name="w2_sraw", align_bytes=64)
        w2_w = keep.tile([P, 2 * H], U8, name="w2_w", align_bytes=64)
        w2_s = keep.tile([P, H], U8, name="w2_s", align_bytes=64)
        wgs_t = keep.tile([P, M], F32, name="wgs_t")
        gain_t = keep.tile([P, 2, 4], F32, name="gain_t")
        gb_rows = keep.tile([P, P], F32, name="gb_rows")
        neg_gb = keep.tile([P, H // P], F32, name="neg_gb")
        ident = keep.tile([P, P], F32, name="ident")
        base_t = [keep.tile([P, S], F32, name="base%d" % i) for i in range(BASES)]
        pages = [keep.tile([P, S], F32, name="page%d" % i) for i in range(PAGES)]
        v_w = keep.tile([P, S], U32, name="v_w", align_bytes=64)
        v_s = keep.tile([P, S], U8, name="v_s", align_bytes=64)
        v2_w = [keep.tile([P, M], U32, name="v2_w%d" % a, align_bytes=64) for a in range(2)]
        v2_s = keep.tile([P, M], U8, name="v2_s", align_bytes=64)
        w1_w = [keep.tile([P, 512], U32, name="w1_w%d" % b, align_bytes=64) for b in range(2)]
        w1_s = [keep.tile([P, 512], U8, name="w1_s%d" % b, align_bytes=64) for b in range(2)]
        w4_w = keep.tile([P, 2, N], U32, name="w4_w", align_bytes=64)
        w4_s = keep.tile([P, 2, N], U8, name="w4_s", align_bytes=64)

        nc.vector.memset(tab2_s[:].bitcast(I32), 0)
        nc.vector.memset(w3_s[:].bitcast(I32), 0)
        nc.gpsimd.memset(gb_rows[:], 0.0)
        nc.vector.memset(tab_s[:].bitcast(I32), 0)
        make_identity(nc, ident[:])
        nc.gpsimd.memset(w2_sraw[:].bitcast(I32), 0)
        for k, page in enumerate(pages):
            (nc.vector if k < 2 else nc.gpsimd).memset(page[:].bitcast(I32), 0)

        load_plane(tab2_s, tab2_scales, range(4))
        nc.sync.dma_start(offs2_t[:], offs2)
        load_plane(w3_s, w3_scales, range(2))
        nc.sync.dma_start(out=tab2_w[0][:], in_=words_of(tab2_words[0]))
        load_plane(w3_s, w3_scales, range(2, 4))
        nc.sync.dma_start(offs_t[:], offs)
        nc.sync.dma_start(out=tab2_w[1][:], in_=words_of(tab2_words[1]))
        w3_all = w3_words.rearrange("a p c i -> p a (c i)").bitcast(I32)
        nc.sync.dma_start(out=w3_head[:], in_=w3_all[:, :, :W3_HEAD])
        load_plane(tab_s, tab_scales, range(4))
        load_plane(w2_sraw, w2_scales, range(4))
        nc.sync.dma_start(out=gb_rows[0 : H // P, :], in_=gb.rearrange("(i p) -> i p", p=P))
        nc.sync.dma_start(pos1_t[:], pos1)
        nc.sync.dma_start(out=wgs_t[:], in_=wgs)
        nc.sync.dma_start(out=w3_rest[:], in_=w3_all[:, :, W3_HEAD:])

        def load_base(i):
            nc.sync.dma_start(out=base_t[i % BASES][:], in_=base[i * P : (i + 1) * P, :])

        def load_w1(b):
            raw = work.tile([P, 4, 512], F32, name="raw", tag="raw")
            nc.sync.dma_start(out=raw[:], in_=w1[:, 512 * b : 512 * (b + 1)].rearrange("(p j) c -> p j c", j=4))
            return raw

        load_base(0)
        nc.sync.dma_start(out=tab_w[:], in_=words_of(tab_words[0]))
        load_base(1)
        w1_raw = [load_w1(0)]
        nc.sync.dma_start(out=w2_raw[:].bitcast(I32), in_=w2_words[0].bitcast(I32))
        load_base(2)
        nc.sync.dma_start(out=gain_t[:], in_=gain.rearrange("(b p t) -> p b t", p=P, t=4))
        w1_raw.append(load_w1(1))
        load_base(3)
        load_base(4)
        w4_raw = keep.tile([P, 2, 4, N], F32, name="w4_raw")
        nc.sync.dma_start(
            out=w4_raw[:].rearrange("p b t n -> p b (t n)"), in_=w4.rearrange("(b p t) n -> p b (t n)", p=P, t=4)
        )
        for i in range(5, BASES):
            load_base(i)

        banks = [psum.tile([P, 512], F32, name="bank%d" % k) for k in range(8)]

        spare = keep.tile([P, 2], F32, name="spare")
        nc.scalar.activation(out=spare[:, 0:1], in_=ident[:, 0:1], func=ACT.Abs_reciprocal_sqrt, bias=1.0)
        gb_ps = banks[7]
        nc.tensor.transpose(gb_ps[:, 0:P], gb_rows[:], ident[:])
        nc.vector.tensor_scalar(neg_gb[:], gb_ps[:, 0 : H // P], -1.0, None, ALU.mult)

        nc.vector.tensor_copy(v2_s[:], tab2_s[:].indirect(offs2_t[:]))
        nc.vector.tensor_copy(v2_w[0][:], tab2_w[0][:].bitcast(U32).indirect(offs2_t[:]))
        nc.vector.tensor_copy(v2_w[1][:], tab2_w[1][:].bitcast(U32).indirect(offs2_t[:]))
        nc.vector.tensor_copy(v_s[:], tab_s[:].indirect(offs_t[:]))

        dist_t = {}

        f_ps, inv = {}, {}

        def soften(i):
            cols = slice(i * P, (i + 1) * P)
            f_ps[i] = banks[i]
            for a in range(2):
                if i * P < W3_HEAD:
                    w3_w = w3_head[:, a, cols]
                else:
                    w3_w = w3_rest[:, a, i * P - W3_HEAD : (i + 1) * P - W3_HEAD]
                nc.tensor.matmul_mx(
                    out=f_ps[i][:], lhsT=w3_w.bitcast(FP8X4), lhsT_scale=w3_s[4 * a :, cols],
                    rhs=v2_w[a][:].bitcast(FP8X4), rhs_scale=v2_s[4 * a :, :], start=(a == 0), stop=(a == 1),
                )
            inv[i] = keep.tile([P, M], F32, name="inv%d" % i)
            nc.scalar.activation(out=inv[i][:], in_=f_ps[i][:], func=ACT.Abs)
            nc.scalar.activation(out=inv[i][:], in_=inv[i][:], func=ACT.Abs_reciprocal_sqrt, bias=1.0)
            nc.scalar.activation(out=inv[i][:], in_=inv[i][:], func=ACT.Square)

        def place(i):
            neg_b = inv[i]
            nc.vector.scalar_tensor_tensor(
                out=neg_b[:], in0=f_ps[i][:], scalar=neg_gb[:, i : i + 1], in1=inv[i][:], op0=ALU.mult, op1=ALU.mult
            )
            page = pages[i % PAGES]
            nc.vector.tensor_tensor(page[:].indirect(pos1_t[:]), neg_b[:], wgs_t[:], ALU.mult)

        def subtract(i):
            page = pages[i % PAGES]
            b, part = divmod(i, 4)
            for half in range(2):
                if part == 0:
                    dist_t[b, half] = work.tile([P, 4, 4, P], F32, name="dist_t", tag="dist", bufs=4)
                x_ps = banks[(0, 2, 0, 2, 4, 0, 4, 4)[i] + half][:].rearrange("j (c r) -> j c r", c=4)
                for step, source in enumerate((base_t[i % BASES], page)):
                    for c in range(4):
                        jc = slice((4 * half + c) * P, (4 * half + c + 1) * P)
                        nc.tensor.matmul(
                            x_ps[:, c, :], source[:, jc], ident[:],
                            start=(step, c) == (0, 0), stop=(step, c) == (1, 3), is_transpose=True,
                        )
                nc.scalar.activation(
                    out=dist_t[b, half][:, :, :, 32 * part : 32 * (part + 1)],
                    in_=x_ps.rearrange("j c (p t) -> j c t p", t=4), func=ACT.Abs,
                )
            if i + BASES < H // P:
                load_base(i + BASES)

        def quantize_w1(b):
            grouped = work.tile([P, 2048], BF16, name="w1_grouped", tag="early", align_bytes=64)
            nc.scalar.copy(
                out=grouped[:].rearrange("p (t m j) -> p m t j", t=4, j=4),
                in_=w1_raw[b][:].rearrange("p j (m t) -> p m t j", t=4),
            )
            nc.vector.quantize_mx(out=w1_w[b][:].bitcast(FP8X4), scales=w1_s[b][:], in_=grouped[:])

        def quantize_w4():
            grouped = work.tile([P, 2048], BF16, name="grouped", tag="grouped", bufs=1, align_bytes=64)
            nc.scalar.copy(
                out=grouped[:].rearrange("p (b n t) -> p b n t", b=2, t=4),
                in_=w4_raw[:].rearrange("p b t n -> p b n t"),
            )
            nc.vector.quantize_mx(
                out=w4_w[:].rearrange("p b n -> p (b n)").bitcast(FP8X4),
                scales=w4_s[:].rearrange("p b n -> p (b n)"), in_=grouped[:],
            )

        blocks = [(0, 0, QW), (0, 256, QW), (0, 512, QW), (1, 0, QW), (0, 768, QW), (1, 256, QW), (1, 512, QW)]
        blocks = blocks + [(1, 768, P), (1, 896, P)]
        units = []
        for k, (b, j0, width) in enumerate(blocks):
            per = 512 // width
            units.extend((k, range(t0, t0 + per)) for t0 in range(0, 4, per))
        a1_ps, a2_ps, d_ps, a1, least, planar, woven, z_w, z_s = ({} for k in range(9))

        def in_parts(tile, width):
            return tile[:].rearrange("p (u j) -> p u j", j=width)

        def multiply(n):
            k, ts = units[n]
            b, j0, width = blocks[k]
            jc = slice(j0, j0 + width)
            a1_ps[n] = in_parts(banks[n % 2], width)
            a2_ps[n] = in_parts(banks[2 + n % 2], width)
            for u, t in enumerate(ts):
                nc.tensor.matmul_mx(
                    out=a1_ps[n][:, u, :], lhsT=w1_w[b][:, t * P : (t + 1) * P].bitcast(FP8X4),
                    lhsT_scale=w1_s[b][:, t * P : (t + 1) * P],
                    rhs=v_w[:, jc].bitcast(FP8X4), rhs_scale=v_s[:, jc], start=True, stop=True,
                )
            for u, t in enumerate(ts):
                c = 512 * b + t * P
                nc.tensor.matmul_mx(
                    out=a2_ps[n][:, u, :], lhsT=w2_w[:, 2 * c : 2 * (c + P)].bitcast(FP4X4),
                    lhsT_scale=w2_s[:, c : c + P],
                    rhs=v_w[:, jc].bitcast(FP8X4), rhs_scale=v_s[:, jc], start=True, stop=True,
                )

        def turn_back(n):
            k, ts = units[n]
            b, j0, width = blocks[k]
            d_ps[n] = in_parts(banks[6 + n % 2], width)
            for u, t in enumerate(ts):
                for c in range(width // P):
                    half, chunk = divmod(j0 // P + c, 4)
                    nc.tensor.transpose(d_ps[n][:, u, c * P : (c + 1) * P], dist_t[b, half][:, chunk, t, :], ident[:])

        def take_least(n):
            width = blocks[units[n][0]][2]
            a1[n] = in_parts(work.tile([P, 512], F32, name="a1", bufs=3), width)
            nc.scalar.copy(out=a1[n], in_=a1_ps[n])
            least[n] = in_parts(work.tile([P, 512], F32, name="least", bufs=3), width)
            nc.vector.tensor_tensor(least[n], a2_ps[n], a1[n], ALU.min)

        def join(n):
            k, ts = units[n]
            b, j0, width = blocks[k]
            if ts[0] == 0:
                planar[k] = work.tile([P, 4, width], BF16, name="planar", bufs=3)
            for u, t in enumerate(ts):
                nc.vector.scalar_tensor_tensor(
                    out=planar[k][:, t, :], in0=least[n][:, u, :], scalar=gain_t[:, b, t : t + 1],
                    in1=d_ps[n][:, u, :], op0=ALU.mult, op1=ALU.add,
                )

        def weave(k):
            width = blocks[k][2]
            woven[k] = work.tile([P, width, 4], BF16, name="woven", align_bytes=64)
            stepped = planar[k][:].rearrange("p t j -> p j t")
            if k < len(blocks) - 2:
                nc.gpsimd.tensor_scalar(woven[k][:], stepped, 1.0, 0.0, ALU.mult, ALU.add)
            elif k == len(blocks) - 1:
                nc.vector.tensor_copy(out=woven[k][:], in_=stepped)
            else:
                nc.scalar.copy(out=woven[k][:], in_=stepped)

        def quantize_z(k):
            b, j0, width = blocks[k]
            codes = work.tile([P, width], U32, name="z_w", bufs=5, align_bytes=64)
            plane = work.tile([P, width], U8, name="z_s", bufs=5, align_bytes=64)
            nc.vector.quantize_mx(
                out=codes[:].bitcast(FP8X4), scales=plane[:], in_=woven[k][:].rearrange("p j t -> p (j t)")
            )
            for c in range(0, width, P):
                z_w[b, j0 + c], z_s[b, j0 + c] = codes[:, c:], plane[:, c:]

        out_v = out.rearrange("(a p) j -> p a j", p=P)

        def score(k):
            b, j0, width = blocks[k]
            y_ps = in_parts(banks[4 + k % 2 if width == QW else 2 * (len(blocks) - 1 - k)], width)[:, 0:2, :]
            for a in range(2):
                for b in range(2):
                    nc.tensor.matmul_mx(
                        out=y_ps[:, a, :], lhsT=w4_w[:, b, a * P : (a + 1) * P].bitcast(FP8X4),
                        lhsT_scale=w4_s[:, b, a * P : (a + 1) * P],
                        rhs=z_w[b, j0][:, :width].bitcast(FP8X4), rhs_scale=z_s[b, j0][:, :width],
                        start=(b == 0), stop=(b == 1),
                    )
            turns = work.tile([P, 2, width], I32, name="turns")
            if j0 < 512:
                staged = work.tile([P, 2, width], F32, name="staged", tag="raw")
                nc.scalar.copy(out=staged[:], in_=y_ps)
                nc.gpsimd.tensor_scalar(turns[:], staged[:], 1.0 / (2.0 * math.pi), 0.0, ALU.mult, ALU.add)
            else:
                nc.vector.tensor_scalar(turns[:], y_ps, 1.0 / (2.0 * math.pi), None, ALU.mult)
            angle = work.tile([P, 2, width], F32, name="angle")
            nc.vector.scalar_tensor_tensor(
                out=angle[:], in0=turns[:], scalar=-2.0 * math.pi, in1=y_ps, op0=ALU.mult, op1=ALU.add
            )
            result = work.tile([P, 2, width], F32, name="result", bufs=4)
            nc.scalar.activation(out=result[:], in_=angle[:], func=ACT.Sin)
            nc.sync.dma_start(out=out_v[:, :, j0 : j0 + width], in_=result[:])

        for i in range(6):
            soften(i)
        nc.vector.tensor_copy(v_w[:], tab_w[:].bitcast(U32).indirect(offs_t[:]))
        nc.vector.tensor_copy(
            out=w2_s[:].rearrange("p (b t m) -> p b t m", b=2, t=4),
            in_=w2_sraw[:].rearrange("p (b m t) -> p b t m", b=2, t=4),
        )
        quantize_w1(0)
        nc.scalar.copy(
            out=w2_w[:].bitcast(U16).rearrange("p (b t m) -> p b t m", b=2, t=4),
            in_=w2_raw[:].bitcast(U16).rearrange("p (b m t) -> p b t m", b=2, t=4),
        )
        soften(6)
        soften(7)
        nc.scalar.activation(out=spare[:, 1:2], in_=inv[7][:, 0:1], func=ACT.Sin)
        for i in range(H // P):
            if i >= PAGES:
                subtract(i - PAGES)
            place(i)
        quantize_w1(1)
        subtract(4)
        quantize_w4()
        subtract(5)
        subtract(6)
        multiply(0)
        turn_back(0)
        multiply(1)
        take_least(0)
        count = len(units)
        ends = {n: k for n, (k, ts) in enumerate(units) if ts[-1] == 3}
        for n in range(count + 2):
            if n + 2 < count:
                multiply(n + 2)
            if n + 1 < count:
                turn_back(n + 1)
                take_least(n + 1)
            if n < count:
                join(n)
            if n == 1:
                subtract(7)
            if n - 1 in ends:
                weave(ends[n - 1])
            if n - 2 in ends:
                quantize_z(ends[n - 2])
                if blocks[ends[n - 2]][0] == 1:
                    score(ends[n - 2])
